import numpy as np
import ml_dtypes


def mxq(x, axis, fmt="e4m3"):
    dtype, down = {"e4m3": (ml_dtypes.float8_e4m3fn, 7), "e5m2": (ml_dtypes.float8_e5m2, 14)}[fmt]
    v = np.moveaxis(np.asarray(x, np.float32).astype(ml_dtypes.bfloat16).astype(np.float64), axis, -1)
    blocks = v.reshape(v.shape[:-1] + (-1, 32))
    amax = np.abs(blocks).max(-1, keepdims=True)
    byte = np.maximum(np.where(amax > 0, np.frexp(amax)[1] - 1 + 127, 0) - down, 1)
    scale = np.exp2(byte - 127.0)
    codes = (blocks / scale).astype(np.float32).astype(dtype).astype(np.float64)
    return np.moveaxis((codes * scale).reshape(v.shape), -1, axis)


WIDE = False


def mx_kscale(k):
    if not WIDE:
        return np.ones(k)
    levels = np.array([10, -10, 5, -5, 0])
    if k % 512:
        return np.exp2(np.random.permutation(np.resize(levels, k // 32))).repeat(32)
    a = np.empty((k // 512, 16))
    for p in range(k // 512):
        a[p, :8] = np.random.permutation(np.resize(levels, 8))
        for g in range(8):
            far = levels[np.abs(levels - a[p, g]) >= 10]
            a[p, g + 8] = far[np.random.randint(len(far))]
    return np.exp2(a.ravel()).repeat(32)


def f64(x):
    return np.asarray(x).astype(np.float64)


def striped(idx):
    return np.tile(idx.reshape(-1, 16).T, (8, 1)).astype(np.uint16)


def unstriped(offs):
    return offs[:16].T.reshape(-1).astype(np.int64)


def striped8(idx):
    return np.concatenate([x.reshape(-1, 16).T for x in idx]).astype(np.uint16)


def runs(offs, k):
    lists = np.stack([offs[16 * r : 16 * r + 16].T.reshape(-1) for r in range(8)]).astype(np.int64)
    return lists[np.arange(k) % 512 // 64]


def pack_weight(w):
    k, n = w.shape
    w = f64(np.asarray(w, np.float32).astype(ml_dtypes.bfloat16)).reshape(k // 32, 32, n)
    amax = np.abs(w).max(1)
    byte = np.clip(np.where(amax > 0, np.frexp(amax)[1] - 1 + 127 - 7, 1), 1, 254)
    scaled = (w * np.exp2(127.0 - byte)[:, None, :]).reshape(k, n).astype(np.float32)
    words = np.ascontiguousarray(scaled.reshape(k // 512, 128, 4, n).transpose(0, 1, 3, 2)).astype(ml_dtypes.float8_e4m3fn).view(np.uint8)
    return words, np.ascontiguousarray(byte.astype(np.uint8).reshape(k // 512, 16, n))


def unpack_weight(words, scales):
    g, p, n, _ = words.shape
    vals = np.ascontiguousarray(words).view(ml_dtypes.float8_e4m3fn).astype(np.float64) * np.repeat(np.exp2(scales.astype(np.float64) - 127.0), 8, axis=1)[..., None]
    return vals.transpose(0, 1, 3, 2).reshape(g * 512, n)

def planes(y):
    n, m = y.shape
    v = y.astype(np.float32).astype(ml_dtypes.bfloat16).astype(np.float64).reshape(n // 32, 32, m)
    top = np.abs(v).max(1)
    byte = np.clip(np.where(top > 0, np.frexp(top)[1] - 1 + 127 - 7, 1), 1, 254)
    codes = (v * np.exp2(127.0 - byte)[:, None, :]).reshape(n, m).astype(np.float32).astype(ml_dtypes.float8_e4m3fn).view(np.uint8)
    words = codes.reshape(n // 512, 128, 4, m).transpose(0, 1, 3, 2)
    return np.ascontiguousarray(words), np.ascontiguousarray(byte.astype(np.uint8).reshape(n // 512, 16, m))


K, T, S, N, H = 512, 2048, 512, 512, 512


def setup_inputs():
    n = np.random.standard_normal
    s = mx_kscale(K)[:, None]
    u = mx_kscale(H)
    packed_xT = pack_weight(n((K, T)) * s)
    packed_w1 = pack_weight(n((K, H)) / np.sqrt(K) / s)
    packed_w2 = pack_weight(n((K, H)) / np.sqrt(K) / s)
    packed_w3 = pack_weight(n((H, N)) / np.sqrt(H) / u[:, None])
    return {
        "x_words": packed_xT[0],
        "x_scales": packed_xT[1],
        "w1_words": packed_w1[0],
        "w1_scales": packed_w1[1],
        "w2_words": packed_w2[0],
        "w2_scales": packed_w2[1],
        "gn": (np.random.uniform(0.5, 1.5, (H, 1)) * u[:, None]).astype(np.float32),
        "w3_words": packed_w3[0],
        "w3_scales": packed_w3[1],
        "offs": striped(np.random.permutation(T)[:S]),
        "two": striped(np.random.permutation(T)[:S]),
        "p1": striped8(np.stack([np.random.permutation(S) for _ in range(8)])),
        "p2": striped8(np.stack([np.random.permutation(S) for _ in range(8)])),
    }


def reference(x_words, x_scales, w1_words, w1_scales, w2_words, w2_scales, gn, w3_words, w3_scales, offs, two, p1, p2):
    xq = unpack_weight(x_words, x_scales)[:, unstriped(offs)]
    y = unpack_weight(w1_words, w1_scales).T @ xq
    k1 = np.exp(-0.5 * ((y - (y[np.arange(H)[:, None], runs(p1, H)])) ** 2))
    x_two = unpack_weight(x_words, x_scales)[:, unstriped(two)]
    c = unpack_weight(w2_words, w2_scales).T @ x_two
    k2 = np.exp(-0.5 * ((y - (y[np.arange(H)[:, None], runs(p2, H)])) ** 2))
    z = f64(gn) * ((k1 * (c[np.arange(H)[:, None], runs(p1, H)]) + k2 * (c[np.arange(H)[:, None], runs(p2, H)])) / (k1 + k2 + 0.5))
    out_0 = unpack_weight(w3_words, w3_scales).T @ mxq(z, 0, "e4m3")
    return (out_0,) + planes(out_0)

@@ -1,0 +1,225 @@
+from contextlib import ExitStack
+
+import concourse.mybir as mybir
+from concourse.masks import make_identity
+
+K, T, S, N, H = 512, 2048, 512, 512, 512
+FLOPS = 3 * 2 * 512 * 512 * 512
+
+F32 = mybir.dt.float32
+BF16 = mybir.dt.bfloat16
+I32 = mybir.dt.int32
+U32 = mybir.dt.uint32
+U16 = mybir.dt.uint16
+U8 = mybir.dt.uint8
+FP8X4 = mybir.dt.float8_e4m3fn_x4
+ACT = mybir.ActivationFunctionType
+ALU = mybir.AluOpType
+
+P = 128
+PACK = 4
+HALF = 256
+CH = 128
+NCH = S // CH
+
+
+def tile_picked_kerndens_none_po_kernel(
+    tc, x_words, x_scales, w1_words, w1_scales, w2_words, w2_scales, gn, w3_words, w3_scales,
+    offs, two, p1, p2, out_0, out_1, out_2,
+):
+    nc = tc.nc
+    with ExitStack() as ctx:
+        keep = ctx.enter_context(tc.tile_pool(name="keep", bufs=1))
+        psum = ctx.enter_context(tc.psum_pool(name="psum", bufs=1))
+
+        def bank(b, shape, name):
+            return psum.tile(shape, F32, name=name, tag="bank%d" % b)
+
+        def words_of(dram):
+            return dram[0].rearrange("p n r -> p (n r)").bitcast(I32)
+
+        def load_list(dram, name):
+            tile = keep.tile([P, S // 16], U16, name=name)
+            nc.sync.dma_start(tile[:], dram)
+            return tile
+
+        def load_scale_rows(queue, tile, dram, first):
+            rows = dram[0].bitcast(I32)
+            for q in range(4):
+                queue.dma_start(
+                    tile[32 * q + first : 32 * q + first + 4, :].bitcast(I32), rows[4 * q : 4 * q + 4, :]
+                )
+
+        def deal(raw, name, dtype):
+            dealt = keep.tile([P, H], dtype, name=name, align_bytes=64)
+            nc.vector.tensor_copy(
+                dealt[:].rearrange("p (t m) -> p t m", t=PACK), raw[:].rearrange("p (m t) -> p t m", t=PACK)
+            )
+            return dealt
+
+        xs = keep.tile([P, T], U8, name="xs", align_bytes=64)
+        w1s_raw = keep.tile([P, H], U8, name="w1s_raw", tag="early", align_bytes=64)
+        w23s_raw = keep.tile([P, H], U8, name="w23s_raw", align_bytes=64)
+        nc.gpsimd.memset(xs[:].bitcast(I32), 0)
+        nc.gpsimd.memset(w1s_raw[:].bitcast(I32), 0)
+
+        offs_sb = load_list(offs, "offs_sb")
+        w1w_raw = keep.tile([P, H], I32, name="w1w_raw", tag="w_raw")
+        nc.sync.dma_start(w1w_raw[:], words_of(w1_words))
+        two_sb = load_list(two, "two_sb")
+        p1_sb = load_list(p1, "p1_sb")
+        p2_sb = load_list(p2, "p2_sb")
+        xw = keep.tile([P, T], U32, name="xw")
+        nc.sync.dma_start(xw[:].bitcast(I32), words_of(x_words))
+        load_scale_rows(nc.scalar, xs, x_scales, 0)
+        load_scale_rows(nc.scalar, w1s_raw, w1_scales, 0)
+
+        ident = keep.tile([P, P], F32, name="ident")
+        make_identity(nc, ident[:])
+        half = keep.tile([P, 1], F32, name="half")
+        nc.gpsimd.memset(half[:], 0.5)
+        nc.gpsimd.memset(w23s_raw[:].bitcast(I32), 0)
+        gain = keep.tile([P, PACK], F32, name="gain")
+        nc.gpsimd.dma_start(gain[:], gn.rearrange("(p t) o -> p (t o)", t=PACK))
+
+        def pick(lst, name, tag):
+            words = keep.tile([P, S], U32, name=name + "_w", tag=tag, align_bytes=64)
+            scales = keep.tile([P, S], U8, name=name + "_s", align_bytes=64)
+            nc.vector.tensor_copy(words[:], xw[:].indirect(lst[:]))
+            nc.vector.tensor_copy(scales[:], xs[:].indirect(lst[:]))
+            return words, scales
+
+        def product(out, w_words, w_scales, first, t, words, scales):
+            cols = slice(t * P, (t + 1) * P)
+            nc.tensor.matmul_mx(
+                out=out, lhsT=w_words[:, cols].bitcast(FP8X4), lhsT_scale=w_scales[first:P, cols],
+                rhs=words.bitcast(FP8X4), rhs_scale=scales, start=True, stop=True,
+            )
+
+        w1w = deal(w1w_raw, "w1w", I32)
+        w2w_raw = keep.tile([P, H], I32, name="w2w_raw", tag="w_raw")
+        nc.sync.dma_start(w2w_raw[:], words_of(w2_words))
+        load_scale_rows(nc.sync, w23s_raw, w2_scales, 0)
+        load_scale_rows(nc.sync, w23s_raw, w3_scales, 4)
+        xa_w, xa_s = pick(offs_sb, "xa", "xa_w")
+        w1s = deal(w1s_raw, "w1s", U8)
+        y_win, y_plain, c_win = [], [], []
+        for t in range(PACK):
+            acc = bank(t, [P, S], "y_acc%d" % t)
+            product(acc[:], w1w, w1s, 0, t, xa_w[:], xa_s[:])
+            win = keep.tile([P, S], F32, name="y_win%d" % t)
+            plain = keep.tile([P, S], F32, name="y_plain%d" % t)
+            nc.scalar.copy(win[:], acc[:])
+            if t == 0:
+                nc.scalar.copy(plain[:], acc[:])
+            else:
+                nc.sync.dma_start(plain[:], win[:])
+            y_win.append(win)
+            y_plain.append(plain)
+
+        xb_w, xb_s = pick(two_sb, "xb", "early")
+        w2w = deal(w2w_raw, "w2w", I32)
+        w3w_raw = keep.tile([P, N], I32, name="w3w_raw", tag="w_raw")
+        nc.sync.dma_start(w3w_raw[:], words_of(w3_words))
+        w23s = deal(w23s_raw, "w23s", U8)
+        c_acc = []
+        for t in range(PACK):
+            acc = bank(PACK + t, [P, S], "c_acc%d" % t)
+            product(acc[:], w2w, w23s, 0, t, xb_w[:], xb_s[:])
+            c_acc.append(acc)
+
+        lists = (p1_sb, p2_sb)
+        den = [bank(j, [P, PACK, P], "den%d" % j) for j in range(NCH)]
+        kern = []
+        for t in range(PACK):
+            diff = keep.tile([P, 2, 2, HALF], F32, name="diff%d" % t)
+            sq = keep.tile([P, 2, 2, HALF], F32, name="sq%d" % t)
+            kt = keep.tile([P, 2, 2, HALF], F32, name="kern%d" % t)
+            for h in range(2):
+                for n in range(2):
+                    nc.vector.tensor_tensor(
+                        diff[:, h, n, :],
+                        y_win[t][:].indirect(lists[n][:, h * HALF // 16 : (h + 1) * HALF // 16]),
+                        y_plain[t][:, h * HALF : (h + 1) * HALF], ALU.subtract,
+                    )
+                nc.scalar.activation(sq[:, h, :, :], diff[:, h, :, :], ACT.Square)
+            nc.scalar.activation(kt[:], sq[:], ACT.Exp, scale=-0.5)
+            kern.append(kt)
+            win = keep.tile([P, S], F32, name="c_win%d" % t)
+            nc.scalar.activation(win[:], c_acc[t][:], ACT.Copy, scale=gain[:, t : t + 1])
+            c_win.append(win)
+            for j in range(NCH):
+                h, o = divmod(j * CH, HALF)
+                for n in range(2):
+                    nc.tensor.matmul(
+                        den[j][:, t, :], lhsT=kt[:, h, n, o : o + CH], rhs=ident[:],
+                        start=(n == 0), stop=(n == 1), is_transpose=True,
+                    )
+
+        w3w = deal(w3w_raw, "w3w", I32)
+
+        logs = keep.tile([P, NCH, H], F32, name="logs")
+        for j in reversed(range(NCH)):
+            nc.scalar.activation(
+                logs[:, j, :].rearrange("s (u p e) -> s u p e", u=2, e=2),
+                den[j][:].rearrange("s (u e) p -> s u p e", u=2),
+                ACT.Ln, bias=half[:],
+            )
+
+        out_codes = keep.tile([P, S], U32, name="out_codes", align_bytes=64)
+        out_scales = keep.tile([P, S], U8, name="out_scales", align_bytes=64)
+        out_rows = out_0.rearrange("(p t) c -> p t c", t=PACK)
+        for j in range(NCH):
+            cols = slice(j * CH, (j + 1) * CH)
+            h, o = divmod(j * CH, HALF)
+            recip = keep.tile([P, H], F32, name="recip%d" % j)
+            nc.scalar.activation(recip[:], logs[:, j, :], ACT.Exp, scale=-1.0)
+
+            num = bank(PACK + j % 2, [P, PACK, P], "num%d" % j)
+            terms = keep.tile([P, PACK, 2, CH], F32, name="terms%d" % j)
+            for t in range(PACK):
+                for n in range(2):
+                    nc.vector.tensor_tensor(
+                        terms[:, t, n, :],
+                        c_win[t][:].indirect(lists[n][:, j * CH // 16 : (j + 1) * CH // 16]),
+                        kern[t][:, h, n, o : o + CH], ALU.mult,
+                    )
+                for n in range(2):
+                    nc.tensor.matmul(
+                        num[:, t, :], lhsT=terms[:, t, n, :], rhs=ident[:],
+                        start=(n == 0), stop=(n == 1), is_transpose=True,
+                    )
+            z_rows = keep.tile([P, H], BF16, name="z_rows%d" % j)
+            nc.vector.tensor_tensor(
+                z_rows[:].rearrange("s (u p e) -> s u p e", u=2, e=2),
+                num[:].rearrange("s (u e) p -> s u p e", u=2),
+                recip[:].rearrange("s (u p e) -> s u p e", u=2, e=2), ALU.mult,
+            )
+            z_turned = bank(PACK + 2, [P, 2, CH], "z_turned%d" % j)
+            pairs = z_rows[:].bitcast(F32)
+            for u in range(2):
+                nc.tensor.transpose(z_turned[:, u, :], pairs[:, u * P : (u + 1) * P], ident[:])
+            z_grouped = keep.tile([P, CH * PACK], BF16, name="z_grouped%d" % j, align_bytes=64)
+            nc.scalar.copy(
+                z_grouped[:].bitcast(F32).rearrange("p (s u) -> p s u", u=2),
+                z_turned[:].rearrange("p u s -> p s u"),
+            )
+            z_codes = keep.tile([P, CH], U32, name="z_codes%d" % j, align_bytes=64)
+            z_scales = keep.tile([P, CH], U8, name="z_scales%d" % j, align_bytes=64)
+            nc.vector.quantize_mx(out=z_codes[:].bitcast(FP8X4), scales=z_scales[:], in_=z_grouped[:])
+
+            acc = bank(j, [P, PACK, CH], "out_acc%d" % j)
+            for t in range(PACK):
+                product(acc[:, t, :], w3w, w23s, 4, t, z_codes[:], z_scales[:])
+            result = keep.tile([P, PACK, CH], F32, name="result%d" % j)
+            nc.scalar.copy(result[:], acc[:])
+            nc.sync.dma_start(out_rows[:, :, cols], result[:])
+            grouped = keep.tile([P, CH * PACK], BF16, name="grouped%d" % j, align_bytes=64)
+            nc.scalar.copy(grouped[:].rearrange("p (s t) -> p s t", t=PACK), acc[:].rearrange("p t s -> p s t"))
+            nc.vector.quantize_mx(out=out_codes[:, cols].bitcast(FP8X4), scales=out_scales[:, cols], in_=grouped[:])
+            nc.sync.dma_start(words_of(out_1)[:, cols], out_codes[:, cols].bitcast(I32))
+
+        scale_rows = out_2[0].bitcast(I32)
+        for q in range(4):
+            queue = nc.sync if q % 2 == 0 else nc.scalar
+            queue.dma_start(scale_rows[4 * q : 4 * q + 4, :], out_scales[32 * q : 32 * q + 4, :].bitcast(I32))

@@ -43,51 +43,55 @@ def tile_picked_kerndens_none_po_kernel(
             nc.sync.dma_start(tile[:], dram)
             return tile
 
-        def load_scale_rows(queue, tile, dram, first):
+        def load_scale_rows(queues, tile, dram, first):
             rows = dram[0].bitcast(I32)
             for q in range(4):
-                queue.dma_start(
+                queues[q].dma_start(
                     tile[32 * q + first : 32 * q + first + 4, :].bitcast(I32), rows[4 * q : 4 * q + 4, :]
                 )
 
         def deal(raw, name, dtype):
             dealt = keep.tile([P, H], dtype, name=name, align_bytes=64)
-            nc.vector.tensor_copy(
+            nc.gpsimd.tensor_copy(
                 dealt[:].rearrange("p (t m) -> p t m", t=PACK), raw[:].rearrange("p (m t) -> p t m", t=PACK)
             )
             return dealt
 
         xs = keep.tile([P, T], U8, name="xs", align_bytes=64)
-        w1s_raw = keep.tile([P, H], U8, name="w1s_raw", tag="early", align_bytes=64)
+        w1s_raw = keep.tile([P, H], U8, name="w1s_raw", align_bytes=64)
         w23s_raw = keep.tile([P, H], U8, name="w23s_raw", align_bytes=64)
         nc.gpsimd.memset(xs[:].bitcast(I32), 0)
-        nc.gpsimd.memset(w1s_raw[:].bitcast(I32), 0)
+        nc.vector.memset(w1s_raw[:].bitcast(I32), 0)
+        nc.vector.memset(w23s_raw[:].bitcast(I32), 0)
 
         offs_sb = load_list(offs, "offs_sb")
-        w1w_raw = keep.tile([P, H], I32, name="w1w_raw", tag="w_raw")
-        nc.sync.dma_start(w1w_raw[:], words_of(w1_words))
         two_sb = load_list(two, "two_sb")
-        p1_sb = load_list(p1, "p1_sb")
-        p2_sb = load_list(p2, "p2_sb")
+        load_scale_rows([nc.sync] * 4, xs, x_scales, 0)
+        w1w_raw = keep.tile([P, H], I32, name="w1w_raw")
+        nc.sync.dma_start(w1w_raw[:], words_of(w1_words))
         xw = keep.tile([P, T], U32, name="xw")
         nc.sync.dma_start(xw[:].bitcast(I32), words_of(x_words))
-        load_scale_rows(nc.scalar, xs, x_scales, 0)
-        load_scale_rows(nc.scalar, w1s_raw, w1_scales, 0)
+        load_scale_rows([nc.sync] * 4, w1s_raw, w1_scales, 0)
+        p1_sb = load_list(p1, "p1_sb")
+        p2_sb = load_list(p2, "p2_sb")
+        gain = keep.tile([P, PACK], F32, name="gain")
+        nc.sync.dma_start(gain[:], gn.rearrange("(p t) o -> p (t o)", t=PACK))
+        w2w_raw = keep.tile([P, H], I32, name="w2w_raw")
+        nc.sync.dma_start(w2w_raw[:], words_of(w2_words))
+        w3w_raw = keep.tile([P, N], I32, name="w3w_raw")
+        nc.sync.dma_start(w3w_raw[:], words_of(w3_words))
+        load_scale_rows([nc.sync] * 4, w23s_raw, w2_scales, 0)
+        load_scale_rows([nc.sync] * 4, w23s_raw, w3_scales, 4)
 
         ident = keep.tile([P, P], F32, name="ident")
         make_identity(nc, ident[:])
         half = keep.tile([P, 1], F32, name="half")
         nc.gpsimd.memset(half[:], 0.5)
-        nc.gpsimd.memset(w23s_raw[:].bitcast(I32), 0)
-        gain = keep.tile([P, PACK], F32, name="gain")
-        nc.gpsimd.dma_start(gain[:], gn.rearrange("(p t) o -> p (t o)", t=PACK))
 
-        def pick(lst, name, tag):
-            words = keep.tile([P, S], U32, name=name + "_w", tag=tag, align_bytes=64)
-            scales = keep.tile([P, S], U8, name=name + "_s", align_bytes=64)
-            nc.vector.tensor_copy(words[:], xw[:].indirect(lst[:]))
-            nc.vector.tensor_copy(scales[:], xs[:].indirect(lst[:]))
-            return words, scales
+        def pick(table, lst, name, dtype, tag):
+            picked = keep.tile([P, S], dtype, name=name, tag=tag, align_bytes=64)
+            nc.vector.tensor_copy(picked[:], table[:].indirect(lst[:]))
+            return picked
 
         def product(out, w_words, w_scales, first, t, words, scales):
             cols = slice(t * P, (t + 1) * P)
@@ -96,31 +100,27 @@ def tile_picked_kerndens_none_po_kernel(
                 rhs=words.bitcast(FP8X4), rhs_scale=scales, start=True, stop=True,
             )
 
+        xa_s = pick(xs, offs_sb, "xa_s", U8, "xa_s")
+        xb_s = pick(xs, two_sb, "xb_s", U8, "xb_s")
         w1w = deal(w1w_raw, "w1w", I32)
-        w2w_raw = keep.tile([P, H], I32, name="w2w_raw", tag="w_raw")
-        nc.sync.dma_start(w2w_raw[:], words_of(w2_words))
-        load_scale_rows(nc.sync, w23s_raw, w2_scales, 0)
-        load_scale_rows(nc.sync, w23s_raw, w3_scales, 4)
-        xa_w, xa_s = pick(offs_sb, "xa", "xa_w")
         w1s = deal(w1s_raw, "w1s", U8)
-        y_win, y_plain, c_win = [], [], []
+        xa_w = pick(xw, offs_sb, "xa_w", U32, "xa_w")
+
+        y_win = [keep.tile([P, S if t == 0 else 2 * S], F32, name="y_win%d" % t) for t in range(PACK)]
+        y_last = keep.tile([P, S], F32, name="y_last", tag="late")
+        y_plain = [y_win[t + 1][:, S:] for t in range(PACK - 1)] + [y_last[:]]
         for t in range(PACK):
             acc = bank(t, [P, S], "y_acc%d" % t)
             product(acc[:], w1w, w1s, 0, t, xa_w[:], xa_s[:])
-            win = keep.tile([P, S], F32, name="y_win%d" % t)
-            plain = keep.tile([P, S], F32, name="y_plain%d" % t)
-            nc.scalar.copy(win[:], acc[:])
+            nc.scalar.copy(y_win[t][:, :S], acc[:])
             if t == 0:
-                nc.scalar.copy(plain[:], acc[:])
+                nc.vector.tensor_copy(y_plain[t], y_win[t][:, :S])
             else:
-                nc.sync.dma_start(plain[:], win[:])
-            y_win.append(win)
-            y_plain.append(plain)
+                nc.sync.dma_start(y_plain[t], y_win[t][:, :S])
 
-        xb_w, xb_s = pick(two_sb, "xb", "early")
+        xb_w = pick(xw, two_sb, "xb_w", U32, "xb_w")
         w2w = deal(w2w_raw, "w2w", I32)
-        w3w_raw = keep.tile([P, N], I32, name="w3w_raw", tag="w_raw")
-        nc.sync.dma_start(w3w_raw[:], words_of(w3_words))
+        w3w = deal(w3w_raw, "w3w", I32)
         w23s = deal(w23s_raw, "w23s", U8)
         c_acc = []
         for t in range(PACK):
@@ -129,73 +129,81 @@ def tile_picked_kerndens_none_po_kernel(
             c_acc.append(acc)
 
         lists = (p1_sb, p2_sb)
-        den = [bank(j, [P, PACK, P], "den%d" % j) for j in range(NCH)]
-        kern = []
+        den = [bank(t, [P, NCH, P], "den%d" % t) for t in range(PACK)]
+        kern, c_win = [], []
         for t in range(PACK):
-            diff = keep.tile([P, 2, 2, HALF], F32, name="diff%d" % t)
-            sq = keep.tile([P, 2, 2, HALF], F32, name="sq%d" % t)
-            kt = keep.tile([P, 2, 2, HALF], F32, name="kern%d" % t)
-            for h in range(2):
-                for n in range(2):
+            diff = keep.tile([P, 2, S], F32, name="diff%d" % t, tag="diff%d" % t)
+            sq = keep.tile([P, 2, S], F32, name="sq%d" % t, tag="sq%d" % t)
+            kt = keep.tile([P, 2, S], F32, name="kern%d" % t)
+            piece = HALF if t == 0 else S
+            for n in range(2):
+                for a in range(0, S, piece):
                     nc.vector.tensor_tensor(
-                        diff[:, h, n, :],
-                        y_win[t][:].indirect(lists[n][:, h * HALF // 16 : (h + 1) * HALF // 16]),
-                        y_plain[t][:, h * HALF : (h + 1) * HALF], ALU.subtract,
+                        diff[:, n, a : a + piece],
+                        y_win[t][:].indirect(lists[n][:, a // 16 : (a + piece) // 16]),
+                        y_plain[t][:, a : a + piece], ALU.subtract,
                     )
-                nc.scalar.activation(sq[:, h, :, :], diff[:, h, :, :], ACT.Square)
-            nc.scalar.activation(kt[:], sq[:], ACT.Exp, scale=-0.5)
+                nc.scalar.activation(sq[:, n, :], diff[:, n, :], ACT.Square)
+            for n in range(2):
+                nc.scalar.activation(kt[:, n, :], sq[:, n, :], ACT.Exp, scale=-0.5)
             kern.append(kt)
-            win = keep.tile([P, S], F32, name="c_win%d" % t)
+            win = keep.tile([P, S], F32, name="c_win%d" % t, tag="diff%d" % t)
             nc.scalar.activation(win[:], c_acc[t][:], ACT.Copy, scale=gain[:, t : t + 1])
             c_win.append(win)
             for j in range(NCH):
-                h, o = divmod(j * CH, HALF)
                 for n in range(2):
                     nc.tensor.matmul(
-                        den[j][:, t, :], lhsT=kt[:, h, n, o : o + CH], rhs=ident[:],
+                        den[t][:, j, :], lhsT=kt[:, n, j * CH : (j + 1) * CH], rhs=ident[:],
                         start=(n == 0), stop=(n == 1), is_transpose=True,
                     )
 
-        w3w = deal(w3w_raw, "w3w", I32)
+        logs = keep.tile([P, NCH, PACK, P], F32, name="logs", tag="sq%d" % (PACK - 1))
+        for t in range(PACK):
+            nc.scalar.activation(logs[:, :, t, :], den[t][:], ACT.Ln, bias=half[:])
 
-        logs = keep.tile([P, NCH, H], F32, name="logs")
-        for j in reversed(range(NCH)):
-            nc.scalar.activation(
-                logs[:, j, :].rearrange("s (u p e) -> s u p e", u=2, e=2),
-                den[j][:].rearrange("s (u e) p -> s u p e", u=2),
-                ACT.Ln, bias=half[:],
-            )
+        num = [bank(j, [P, PACK, P], "num%d" % j) for j in range(NCH)]
+
+        def weigh(terms, t, a, b):
+            for n in range(2):
+                nc.vector.tensor_tensor(
+                    terms[:, n, :], c_win[t][:].indirect(lists[n][:, a // 16 : b // 16]), kern[t][:, n, a:b], ALU.mult
+                )
+            for j in range(a // CH, b // CH):
+                for n in range(2):
+                    nc.tensor.matmul(
+                        num[j][:, t, :], lhsT=terms[:, n, j * CH - a : (j + 1) * CH - a], rhs=ident[:],
+                        start=(n == 0), stop=(n == 1), is_transpose=True,
+                    )
+
+        cut = S - CH
+        first = keep.tile([P, PACK * 2 * cut + 4 * CH], F32, name="first", tag="late")
+        for t in range(PACK):
+            weigh(first[:, 2 * cut * t : 2 * cut * (t + 1)].rearrange("p (n s) -> p n s", n=2), t, 0, cut)
+        for t in range(2):
+            base = PACK * 2 * cut + 2 * CH * t
+            weigh(first[:, base : base + 2 * CH].rearrange("p (n s) -> p n s", n=2), t, cut, S)
 
         out_codes = keep.tile([P, S], U32, name="out_codes", align_bytes=64)
         out_scales = keep.tile([P, S], U8, name="out_scales", align_bytes=64)
         out_rows = out_0.rearrange("(p t) c -> p t c", t=PACK)
+        out_acc = []
         for j in range(NCH):
-            cols = slice(j * CH, (j + 1) * CH)
-            h, o = divmod(j * CH, HALF)
-            recip = keep.tile([P, H], F32, name="recip%d" % j)
-            nc.scalar.activation(recip[:], logs[:, j, :], ACT.Exp, scale=-1.0)
+            recip = keep.tile([P, H], F32, name="recip%d" % j, tag="recip%d" % j)
+            nc.scalar.activation(
+                recip[:].rearrange("s (u p e) -> s u p e", u=2, e=2),
+                logs[:, j, :, :].rearrange("s (u e) p -> s u p e", u=2), ACT.Exp, scale=-1.0,
+            )
 
-            num = bank(PACK + j % 2, [P, PACK, P], "num%d" % j)
-            terms = keep.tile([P, PACK, 2, CH], F32, name="terms%d" % j)
-            for t in range(PACK):
-                for n in range(2):
-                    nc.vector.tensor_tensor(
-                        terms[:, t, n, :],
-                        c_win[t][:].indirect(lists[n][:, j * CH // 16 : (j + 1) * CH // 16]),
-                        kern[t][:, h, n, o : o + CH], ALU.mult,
-                    )
-                for n in range(2):
-                    nc.tensor.matmul(
-                        num[:, t, :], lhsT=terms[:, t, n, :], rhs=ident[:],
-                        start=(n == 0), stop=(n == 1), is_transpose=True,
-                    )
             z_rows = keep.tile([P, H], BF16, name="z_rows%d" % j)
             nc.vector.tensor_tensor(
                 z_rows[:].rearrange("s (u p e) -> s u p e", u=2, e=2),
-                num[:].rearrange("s (u e) p -> s u p e", u=2),
+                num[j][:].rearrange("s (u e) p -> s u p e", u=2),
                 recip[:].rearrange("s (u p e) -> s u p e", u=2, e=2), ALU.mult,
             )
-            z_turned = bank(PACK + 2, [P, 2, CH], "z_turned%d" % j)
+            if j < 2:
+                last = keep.tile([P, 2, CH], F32, name="last%d" % j, tag="recip%d" % j)
+                weigh(last[:], 2 + j, cut, S)
+            z_turned = bank(PACK + j, [P, 2, CH], "z_turned%d" % j)
             pairs = z_rows[:].bitcast(F32)
             for u in range(2):
                 nc.tensor.transpose(z_turned[:, u, :], pairs[:, u * P : (u + 1) * P], ident[:])
@@ -211,11 +219,17 @@ def tile_picked_kerndens_none_po_kernel(
             acc = bank(j, [P, PACK, CH], "out_acc%d" % j)
             for t in range(PACK):
                 product(acc[:, t, :], w3w, w23s, 4, t, z_codes[:], z_scales[:])
+            out_acc.append(acc)
+
+        for j in range(NCH):
+            cols = slice(j * CH, (j + 1) * CH)
             result = keep.tile([P, PACK, CH], F32, name="result%d" % j)
-            nc.scalar.copy(result[:], acc[:])
+            nc.scalar.copy(result[:], out_acc[j][:])
             nc.sync.dma_start(out_rows[:, :, cols], result[:])
             grouped = keep.tile([P, CH * PACK], BF16, name="grouped%d" % j, align_bytes=64)
-            nc.scalar.copy(grouped[:].rearrange("p (s t) -> p s t", t=PACK), acc[:].rearrange("p t s -> p s t"))
+            nc.vector.tensor_copy(
+                grouped[:].rearrange("p (s t) -> p s t", t=PACK), result[:].rearrange("p t s -> p s t")
+            )
             nc.vector.quantize_mx(out=out_codes[:, cols].bitcast(FP8X4), scales=out_scales[:, cols], in_=grouped[:])
             nc.sync.dma_start(words_of(out_1)[:, cols], out_codes[:, cols].bitcast(I32))
 

@@ -52,7 +52,7 @@ def tile_picked_kerndens_none_po_kernel(
 
         def deal(raw, name, dtype):
             dealt = keep.tile([P, H], dtype, name=name, align_bytes=64)
-            nc.gpsimd.tensor_copy(
+            nc.vector.tensor_copy(
                 dealt[:].rearrange("p (t m) -> p t m", t=PACK), raw[:].rearrange("p (m t) -> p t m", t=PACK)
             )
             return dealt
@@ -114,13 +114,12 @@ def tile_picked_kerndens_none_po_kernel(
             product(acc[:], w1w, w1s, 0, t, xa_w[:], xa_s[:])
             nc.scalar.copy(y_win[t][:, :S], acc[:])
             if t == 0:
-                nc.vector.tensor_copy(y_plain[t], y_win[t][:, :S])
+                nc.scalar.copy(y_plain[t], acc[:])
             else:
                 nc.sync.dma_start(y_plain[t], y_win[t][:, :S])
 
         xb_w = pick(xw, two_sb, "xb_w", U32, "xb_w")
         w2w = deal(w2w_raw, "w2w", I32)
-        w3w = deal(w3w_raw, "w3w", I32)
         w23s = deal(w23s_raw, "w23s", U8)
         c_acc = []
         for t in range(PACK):
@@ -157,6 +156,8 @@ def tile_picked_kerndens_none_po_kernel(
                         start=(n == 0), stop=(n == 1), is_transpose=True,
                     )
 
+        w3w = deal(w3w_raw, "w3w", I32)
+
         logs = keep.tile([P, NCH, PACK, P], F32, name="logs", tag="sq%d" % (PACK - 1))
         for t in range(PACK):
             nc.scalar.activation(logs[:, :, t, :], den[t][:], ACT.Ln, bias=half[:])
@@ -176,12 +177,13 @@ def tile_picked_kerndens_none_po_kernel(
                     )
 
         cut = S - CH
-        first = keep.tile([P, PACK * 2 * cut + 4 * CH], F32, name="first", tag="late")
-        for t in range(PACK):
-            weigh(first[:, 2 * cut * t : 2 * cut * (t + 1)].rearrange("p (n s) -> p n s", n=2), t, 0, cut)
-        for t in range(2):
-            base = PACK * 2 * cut + 2 * CH * t
-            weigh(first[:, base : base + 2 * CH].rearrange("p (n s) -> p n s", n=2), t, cut, S)
+        first = keep.tile([P, PACK * 2 * cut + 2 * CH], F32, name="first", tag="late")
+        base = 0
+        for t, a, b in (
+            [(t, 0, HALF) for t in range(PACK)] + [(t, HALF, cut) for t in range(PACK)] + [(0, cut, S)]
+        ):
+            weigh(first[:, base : base + 2 * (b - a)].rearrange("p (n s) -> p n s", n=2), t, a, b)
+            base = base + 2 * (b - a)
 
         out_codes = keep.tile([P, S], U32, name="out_codes", align_bytes=64)
         out_scales = keep.tile([P, S], U8, name="out_scales", align_bytes=64)
@@ -200,9 +202,9 @@ def tile_picked_kerndens_none_po_kernel(
                 num[j][:].rearrange("s (u e) p -> s u p e", u=2),
                 recip[:].rearrange("s (u p e) -> s u p e", u=2, e=2), ALU.mult,
             )
-            if j < 2:
+            if j < NCH - 1:
                 last = keep.tile([P, 2, CH], F32, name="last%d" % j, tag="recip%d" % j)
-                weigh(last[:], 2 + j, cut, S)
+                weigh(last[:], 1 + j, cut, S)
             z_turned = bank(PACK + j, [P, 2, CH], "z_turned%d" % j)
             pairs = z_rows[:].bitcast(F32)
             for u in range(2):

@@ -50,38 +50,39 @@ def tile_picked_kerndens_none_po_kernel(
                     tile[32 * q + first : 32 * q + first + 4, :].bitcast(I32), rows[4 * q : 4 * q + 4, :]
                 )
 
-        def deal(raw, name, dtype):
+        def deal(raw, name, dtype, run):
             dealt = keep.tile([P, H], dtype, name=name, align_bytes=64)
             nc.vector.tensor_copy(
-                dealt[:].rearrange("p (t m) -> p t m", t=PACK), raw[:].rearrange("p (m t) -> p t m", t=PACK)
+                dealt[:].rearrange("p (t c i) -> p c t i", t=PACK, i=run),
+                raw[:].rearrange("p (c i t) -> p c t i", t=PACK, i=run),
             )
             return dealt
 
         xs = keep.tile([P, T], U8, name="xs", align_bytes=64)
-        w1s_raw = keep.tile([P, H], U8, name="w1s_raw", align_bytes=64)
-        w23s_raw = keep.tile([P, H], U8, name="w23s_raw", align_bytes=64)
+        w1s_raw = keep.tile([P, H], U8, name="w1s_raw", tag="early", align_bytes=64)
+        w23s_raw = keep.tile([P, H], U8, name="w23s_raw", tag="diff0_0", align_bytes=64)
         nc.gpsimd.memset(xs[:].bitcast(I32), 0)
         nc.vector.memset(w1s_raw[:].bitcast(I32), 0)
         nc.vector.memset(w23s_raw[:].bitcast(I32), 0)
 
+        w1w_raw = keep.tile([P, H], I32, name="w1w_raw")
+        nc.sync.dma_start(w1w_raw[:], words_of(w1_words))
         offs_sb = load_list(offs, "offs_sb")
         two_sb = load_list(two, "two_sb")
         load_scale_rows([nc.sync] * 4, xs, x_scales, 0)
-        w1w_raw = keep.tile([P, H], I32, name="w1w_raw")
-        nc.sync.dma_start(w1w_raw[:], words_of(w1_words))
         xw = keep.tile([P, T], U32, name="xw")
         nc.sync.dma_start(xw[:].bitcast(I32), words_of(x_words))
         load_scale_rows([nc.sync] * 4, w1s_raw, w1_scales, 0)
         p1_sb = load_list(p1, "p1_sb")
         p2_sb = load_list(p2, "p2_sb")
-        gain = keep.tile([P, PACK], F32, name="gain")
-        nc.sync.dma_start(gain[:], gn.rearrange("(p t) o -> p (t o)", t=PACK))
-        w2w_raw = keep.tile([P, H], I32, name="w2w_raw")
+        w2w_raw = keep.tile([P, H], I32, name="w2w_raw", tag="diff0_1", align_bytes=64)
         nc.sync.dma_start(w2w_raw[:], words_of(w2_words))
-        w3w_raw = keep.tile([P, N], I32, name="w3w_raw")
-        nc.sync.dma_start(w3w_raw[:], words_of(w3_words))
         load_scale_rows([nc.sync] * 4, w23s_raw, w2_scales, 0)
         load_scale_rows([nc.sync] * 4, w23s_raw, w3_scales, 4)
+        gain = keep.tile([P, PACK], F32, name="gain")
+        nc.sync.dma_start(gain[:], gn.rearrange("(p t) o -> p (t o)", t=PACK))
+        w3w_raw = keep.tile([P, N], I32, name="w3w_raw")
+        nc.sync.dma_start(w3w_raw[:], words_of(w3_words))
 
         ident = keep.tile([P, P], F32, name="ident")
         make_identity(nc, ident[:])
@@ -102,9 +103,9 @@ def tile_picked_kerndens_none_po_kernel(
 
         xa_s = pick(xs, offs_sb, "xa_s", U8, "xa_s")
         xb_s = pick(xs, two_sb, "xb_s", U8, "xb_s")
-        w1w = deal(w1w_raw, "w1w", I32)
-        w1s = deal(w1s_raw, "w1s", U8)
+        w1w = deal(w1w_raw, "w1w", I32, 4)
         xa_w = pick(xw, offs_sb, "xa_w", U32, "xa_w")
+        w1s = deal(w1s_raw, "w1s", U8, 16)
 
         y_win = [keep.tile([P, S if t == 0 else 2 * S], F32, name="y_win%d" % t) for t in range(PACK)]
         y_last = keep.tile([P, S], F32, name="y_last", tag="late")
@@ -118,9 +119,9 @@ def tile_picked_kerndens_none_po_kernel(
             else:
                 nc.sync.dma_start(y_plain[t], y_win[t][:, :S])
 
-        xb_w = pick(xw, two_sb, "xb_w", U32, "xb_w")
-        w2w = deal(w2w_raw, "w2w", I32)
-        w23s = deal(w23s_raw, "w23s", U8)
+        xb_w = pick(xw, two_sb, "xb_w", U32, "early")
+        w2w = deal(w2w_raw, "w2w", I32, 4)
+        w23s = deal(w23s_raw, "w23s", U8, 16)
         c_acc = []
         for t in range(PACK):
             acc = bank(PACK + t, [P, S], "c_acc%d" % t)
@@ -128,27 +129,28 @@ def tile_picked_kerndens_none_po_kernel(
             c_acc.append(acc)
 
         lists = (p1_sb, p2_sb)
-        den = [bank(t, [P, NCH, P], "den%d" % t) for t in range(PACK)]
-        kern, c_win = [], []
+        den, kern, c_win = [], [], []
         for t in range(PACK):
-            diff = keep.tile([P, 2, S], F32, name="diff%d" % t, tag="diff%d" % t)
             sq = keep.tile([P, 2, S], F32, name="sq%d" % t, tag="sq%d" % t)
             kt = keep.tile([P, 2, S], F32, name="kern%d" % t)
             piece = HALF if t == 0 else S
             for n in range(2):
+                diff = keep.tile([P, S], F32, name="diff%d_%d" % (t, n), tag="diff%d_%d" % (t, n), align_bytes=64)
                 for a in range(0, S, piece):
                     nc.vector.tensor_tensor(
-                        diff[:, n, a : a + piece],
+                        diff[:, a : a + piece],
                         y_win[t][:].indirect(lists[n][:, a // 16 : (a + piece) // 16]),
                         y_plain[t][:, a : a + piece], ALU.subtract,
                     )
-                nc.scalar.activation(sq[:, n, :], diff[:, n, :], ACT.Square)
+                nc.scalar.activation(sq[:, n, :], diff[:], ACT.Square)
+                if n == 0:
+                    win = keep.tile([P, S], F32, name="c_win%d" % t, tag="diff%d_0" % t, align_bytes=64)
+                    nc.scalar.activation(win[:], c_acc[t][:], ACT.Copy, scale=gain[:, t : t + 1])
+                    c_win.append(win)
             for n in range(2):
                 nc.scalar.activation(kt[:, n, :], sq[:, n, :], ACT.Exp, scale=-0.5)
             kern.append(kt)
-            win = keep.tile([P, S], F32, name="c_win%d" % t, tag="diff%d" % t)
-            nc.scalar.activation(win[:], c_acc[t][:], ACT.Copy, scale=gain[:, t : t + 1])
-            c_win.append(win)
+            den.append(bank(PACK + t, [P, NCH, P], "den%d" % t))
             for j in range(NCH):
                 for n in range(2):
                     nc.tensor.matmul(
@@ -156,13 +158,25 @@ def tile_picked_kerndens_none_po_kernel(
                         start=(n == 0), stop=(n == 1), is_transpose=True,
                     )
 
-        w3w = deal(w3w_raw, "w3w", I32)
+        w3w = deal(w3w_raw, "w3w", I32, 4)
 
         logs = keep.tile([P, NCH, PACK, P], F32, name="logs", tag="sq%d" % (PACK - 1))
         for t in range(PACK):
             nc.scalar.activation(logs[:, :, t, :], den[t][:], ACT.Ln, bias=half[:])
 
-        num = [bank(j, [P, PACK, P], "num%d" % j) for j in range(NCH)]
+        def pair_views(j, name, spare):
+            if j < NCH - 1:
+                whole = bank(PACK + j, [P, PACK, P], name)
+                return [(whole[:], 0, 2)]
+            low = bank(PACK + j, [P, 2, P], name + "_low")
+            high = bank(spare, [P, 2, P], name + "_high")
+            return [(low[:], 0, 1), (high[:], 1, 2)]
+
+        def slot(views, t):
+            view, u0, u1 = views[-1] if t >= 2 else views[0]
+            return view[:, t - 2 * u0, :]
+
+        num = [pair_views(j, "num%d" % j, NCH - 1) for j in range(NCH)]
 
         def weigh(terms, t, a, b):
             for n in range(2):
@@ -172,15 +186,15 @@ def tile_picked_kerndens_none_po_kernel(
             for j in range(a // CH, b // CH):
                 for n in range(2):
                     nc.tensor.matmul(
-                        num[j][:, t, :], lhsT=terms[:, n, j * CH - a : (j + 1) * CH - a], rhs=ident[:],
+                        slot(num[j], t), lhsT=terms[:, n, j * CH - a : (j + 1) * CH - a], rhs=ident[:],
                         start=(n == 0), stop=(n == 1), is_transpose=True,
                     )
 
         cut = S - CH
-        first = keep.tile([P, PACK * 2 * cut + 2 * CH], F32, name="first", tag="late")
+        first = keep.tile([P, PACK * 2 * cut + 4 * CH], F32, name="first", tag="late")
         base = 0
         for t, a, b in (
-            [(t, 0, HALF) for t in range(PACK)] + [(t, HALF, cut) for t in range(PACK)] + [(0, cut, S)]
+            [(t, 0, HALF) for t in range(PACK)] + [(t, HALF, cut) for t in range(PACK)] + [(0, cut, S), (1, cut, S)]
         ):
             weigh(first[:, base : base + 2 * (b - a)].rearrange("p (n s) -> p n s", n=2), t, a, b)
             base = base + 2 * (b - a)
@@ -195,20 +209,21 @@ def tile_picked_kerndens_none_po_kernel(
                 recip[:].rearrange("s (u p e) -> s u p e", u=2, e=2),
                 logs[:, j, :, :].rearrange("s (u e) p -> s u p e", u=2), ACT.Exp, scale=-1.0,
             )
-
             z_rows = keep.tile([P, H], BF16, name="z_rows%d" % j)
-            nc.vector.tensor_tensor(
-                z_rows[:].rearrange("s (u p e) -> s u p e", u=2, e=2),
-                num[j][:].rearrange("s (u e) p -> s u p e", u=2),
-                recip[:].rearrange("s (u p e) -> s u p e", u=2, e=2), ALU.mult,
-            )
-            if j < NCH - 1:
-                last = keep.tile([P, 2, CH], F32, name="last%d" % j, tag="recip%d" % j)
-                weigh(last[:], 1 + j, cut, S)
-            z_turned = bank(PACK + j, [P, 2, CH], "z_turned%d" % j)
+            z_turned = bank(j % (NCH - 1), [P, 2, CH], "z_turned%d" % j)
             pairs = z_rows[:].bitcast(F32)
-            for u in range(2):
-                nc.tensor.transpose(z_turned[:, u, :], pairs[:, u * P : (u + 1) * P], ident[:])
+            for view, u0, u1 in num[j]:
+                span = slice(u0 * HALF, u1 * HALF)
+                nc.vector.tensor_tensor(
+                    z_rows[:, span].rearrange("s (u p e) -> s u p e", p=P, e=2),
+                    view.rearrange("s (u e) p -> s u p e", e=2),
+                    recip[:, span].rearrange("s (u p e) -> s u p e", p=P, e=2), ALU.mult,
+                )
+                for u in range(u0, u1):
+                    nc.tensor.transpose(z_turned[:, u, :], pairs[:, u * P : (u + 1) * P], ident[:])
+            if j < 2:
+                last = keep.tile([P, 2, CH], F32, name="last%d" % j, tag="recip%d" % j)
+                weigh(last[:], 2 + j, cut, S)
             z_grouped = keep.tile([P, CH * PACK], BF16, name="z_grouped%d" % j, align_bytes=64)
             nc.scalar.copy(
                 z_grouped[:].bitcast(F32).rearrange("p (s u) -> p s u", u=2),
@@ -218,15 +233,16 @@ def tile_picked_kerndens_none_po_kernel(
             z_scales = keep.tile([P, CH], U8, name="z_scales%d" % j, align_bytes=64)
             nc.vector.quantize_mx(out=z_codes[:].bitcast(FP8X4), scales=z_scales[:], in_=z_grouped[:])
 
-            acc = bank(j, [P, PACK, CH], "out_acc%d" % j)
+            acc = pair_views(j, "out_acc%d" % j, NCH - 1)
             for t in range(PACK):
-                product(acc[:, t, :], w3w, w23s, 4, t, z_codes[:], z_scales[:])
+                product(slot(acc, t), w3w, w23s, 4, t, z_codes[:], z_scales[:])
             out_acc.append(acc)
 
         for j in range(NCH):
             cols = slice(j * CH, (j + 1) * CH)
             result = keep.tile([P, PACK, CH], F32, name="result%d" % j)
-            nc.scalar.copy(result[:], out_acc[j][:])
+            for view, u0, u1 in out_acc[j]:
+                nc.scalar.copy(result[:, 2 * u0 : 2 * u1, :], view)
             nc.sync.dma_start(out_rows[:, :, cols], result[:])
             grouped = keep.tile([P, CH * PACK], BF16, name="grouped%d" % j, align_bytes=64)
             nc.vector.tensor_copy(

from contextlib import ExitStack

import concourse.mybir as mybir
from concourse.masks import make_identity

K, T, S, N, H = 512, 2048, 512, 512, 512
FLOPS = 3 * 2 * 512 * 512 * 512

F32 = mybir.dt.float32
BF16 = mybir.dt.bfloat16
I32 = mybir.dt.int32
U32 = mybir.dt.uint32
U16 = mybir.dt.uint16
U8 = mybir.dt.uint8
FP8X4 = mybir.dt.float8_e4m3fn_x4
ACT = mybir.ActivationFunctionType
ALU = mybir.AluOpType

P = 128
PACK = 4
HALF = 256
CH = 128
NCH = S // CH


def tile_picked_kerndens_none_po_kernel(
    tc, x_words, x_scales, w1_words, w1_scales, w2_words, w2_scales, gn, w3_words, w3_scales,
    offs, two, p1, p2, out_0, out_1, out_2,
):
    nc = tc.nc
    with ExitStack() as ctx:
        keep = ctx.enter_context(tc.tile_pool(name="keep", bufs=1))
        psum = ctx.enter_context(tc.psum_pool(name="psum", bufs=1))

        def bank(b, shape, name):
            return psum.tile(shape, F32, name=name, tag="bank%d" % b)

        def words_of(dram):
            return dram[0].rearrange("p n r -> p (n r)").bitcast(I32)

        def load_list(dram, name):
            tile = keep.tile([P, S // 16], U16, name=name)
            nc.sync.dma_start(tile[:], dram)
            return tile

        def load_scale_rows(queues, tile, dram, first):
            rows = dram[0].bitcast(I32)
            for q in range(4):
                queues[q].dma_start(
                    tile[32 * q + first : 32 * q + first + 4, :].bitcast(I32), rows[4 * q : 4 * q + 4, :]
                )

        def deal(raw, name, dtype, run):
            dealt = keep.tile([P, H], dtype, name=name, align_bytes=64)
            nc.vector.tensor_copy(
                dealt[:].rearrange("p (t c i) -> p c t i", t=PACK, i=run),
                raw[:].rearrange("p (c i t) -> p c t i", t=PACK, i=run),
            )
            return dealt

        xs = keep.tile([P, T], U8, name="xs", align_bytes=64)
        w1s_raw = keep.tile([P, H], U8, name="w1s_raw", tag="early", align_bytes=64)
        w23s_raw = keep.tile([P, H], U8, name="w23s_raw", tag="diff0_0", align_bytes=64)
        nc.gpsimd.memset(xs[:].bitcast(I32), 0)
        nc.vector.memset(w1s_raw[:].bitcast(I32), 0)
        nc.vector.memset(w23s_raw[:].bitcast(I32), 0)

        w1w_raw = keep.tile([P, H], I32, name="w1w_raw")
        nc.sync.dma_start(w1w_raw[:], words_of(w1_words))
        offs_sb = load_list(offs, "offs_sb")
        two_sb = load_list(two, "two_sb")
        load_scale_rows([nc.sync] * 4, xs, x_scales, 0)
        xw = keep.tile([P, T], U32, name="xw")
        nc.sync.dma_start(xw[:].bitcast(I32), words_of(x_words))
        load_scale_rows([nc.sync] * 4, w1s_raw, w1_scales, 0)
        p1_sb = load_list(p1, "p1_sb")
        p2_sb = load_list(p2, "p2_sb")
        w2w_raw = keep.tile([P, H], I32, name="w2w_raw", tag="diff0_1", align_bytes=64)
        nc.sync.dma_start(w2w_raw[:], words_of(w2_words))
        load_scale_rows([nc.sync] * 4, w23s_raw, w2_scales, 0)
        load_scale_rows([nc.sync] * 4, w23s_raw, w3_scales, 4)
        gain = keep.tile([P, PACK], F32, name="gain")
        nc.sync.dma_start(gain[:], gn.rearrange("(p t) o -> p (t o)", t=PACK))
        w3w_raw = keep.tile([P, N], I32, name="w3w_raw")
        nc.sync.dma_start(w3w_raw[:], words_of(w3_words))

        ident = keep.tile([P, P], F32, name="ident")
        make_identity(nc, ident[:])
        half = keep.tile([P, 1], F32, name="half")
        nc.gpsimd.memset(half[:], 0.5)

        def pick(table, lst, name, dtype, tag):
            picked = keep.tile([P, S], dtype, name=name, tag=tag, align_bytes=64)
            nc.vector.tensor_copy(picked[:], table[:].indirect(lst[:]))
            return picked

        def product(out, w_words, w_scales, first, t, words, scales):
            cols = slice(t * P, (t + 1) * P)
            nc.tensor.matmul_mx(
                out=out, lhsT=w_words[:, cols].bitcast(FP8X4), lhsT_scale=w_scales[first:P, cols],
                rhs=words.bitcast(FP8X4), rhs_scale=scales, start=True, stop=True,
            )

        xa_s = pick(xs, offs_sb, "xa_s", U8, "xa_s")
        xb_s = pick(xs, two_sb, "xb_s", U8, "xb_s")
        w1w = deal(w1w_raw, "w1w", I32, 4)
        xa_w = pick(xw, offs_sb, "xa_w", U32, "xa_w")
        w1s = deal(w1s_raw, "w1s", U8, 16)

        y_win = [keep.tile([P, S if t == 0 else 2 * S], F32, name="y_win%d" % t) for t in range(PACK)]
        y_last = keep.tile([P, S], F32, name="y_last", tag="late")
        y_plain = [y_win[t + 1][:, S:] for t in range(PACK - 1)] + [y_last[:]]
        for t in range(PACK):
            acc = bank(t, [P, S], "y_acc%d" % t)
            product(acc[:], w1w, w1s, 0, t, xa_w[:], xa_s[:])
            nc.scalar.copy(y_win[t][:, :S], acc[:])
            if t == 0:
                nc.scalar.copy(y_plain[t], acc[:])
            else:
                nc.sync.dma_start(y_plain[t], y_win[t][:, :S])

        xb_w = pick(xw, two_sb, "xb_w", U32, "early")
        w2w = deal(w2w_raw, "w2w", I32, 4)
        w23s = deal(w23s_raw, "w23s", U8, 16)
        c_acc = []
        for t in range(PACK):
            acc = bank(PACK + t, [P, S], "c_acc%d" % t)
            product(acc[:], w2w, w23s, 0, t, xb_w[:], xb_s[:])
            c_acc.append(acc)

        lists = (p1_sb, p2_sb)
        den, kern, c_win = [], [], []
        for t in range(PACK):
            sq = keep.tile([P, 2, S], F32, name="sq%d" % t, tag="sq%d" % t)
            kt = keep.tile([P, 2, S], F32, name="kern%d" % t)
            piece = HALF if t == 0 else S
            for n in range(2):
                diff = keep.tile([P, S], F32, name="diff%d_%d" % (t, n), tag="diff%d_%d" % (t, n), align_bytes=64)
                for a in range(0, S, piece):
                    nc.vector.tensor_tensor(
                        diff[:, a : a + piece],
                        y_win[t][:].indirect(lists[n][:, a // 16 : (a + piece) // 16]),
                        y_plain[t][:, a : a + piece], ALU.subtract,
                    )
                nc.scalar.activation(sq[:, n, :], diff[:], ACT.Square)
                if n == 0:
                    win = keep.tile([P, S], F32, name="c_win%d" % t, tag="diff%d_0" % t, align_bytes=64)
                    nc.scalar.activation(win[:], c_acc[t][:], ACT.Copy, scale=gain[:, t : t + 1])
                    c_win.append(win)
            for n in range(2):
                nc.scalar.activation(kt[:, n, :], sq[:, n, :], ACT.Exp, scale=-0.5)
            kern.append(kt)
            den.append(bank(PACK + t, [P, NCH, P], "den%d" % t))
            for j in range(NCH):
                for n in range(2):
                    nc.tensor.matmul(
                        den[t][:, j, :], lhsT=kt[:, n, j * CH : (j + 1) * CH], rhs=ident[:],
                        start=(n == 0), stop=(n == 1), is_transpose=True,
                    )

        w3w = deal(w3w_raw, "w3w", I32, 4)

        logs = keep.tile([P, NCH, PACK, P], F32, name="logs", tag="sq%d" % (PACK - 1))
        for t in range(PACK):
            nc.scalar.activation(logs[:, :, t, :], den[t][:], ACT.Ln, bias=half[:])

        def pair_views(j, name, spare):
            if j < NCH - 1:
                whole = bank(PACK + j, [P, PACK, P], name)
                return [(whole[:], 0, 2)]
            low = bank(PACK + j, [P, 2, P], name + "_low")
            high = bank(spare, [P, 2, P], name + "_high")
            return [(low[:], 0, 1), (high[:], 1, 2)]

        def slot(views, t):
            view, u0, u1 = views[-1] if t >= 2 else views[0]
            return view[:, t - 2 * u0, :]

        num = [pair_views(j, "num%d" % j, NCH - 1) for j in range(NCH)]

        def weigh(terms, t, a, b):
            for n in range(2):
                nc.vector.tensor_tensor(
                    terms[:, n, :], c_win[t][:].indirect(lists[n][:, a // 16 : b // 16]), kern[t][:, n, a:b], ALU.mult
                )
            for j in range(a // CH, b // CH):
                for n in range(2):
                    nc.tensor.matmul(
                        slot(num[j], t), lhsT=terms[:, n, j * CH - a : (j + 1) * CH - a], rhs=ident[:],
                        start=(n == 0), stop=(n == 1), is_transpose=True,
                    )

        cut = S - CH
        first = keep.tile([P, PACK * 2 * cut + 4 * CH], F32, name="first", tag="late")
        base = 0
        for t, a, b in (
            [(t, 0, HALF) for t in range(PACK)] + [(t, HALF, cut) for t in range(PACK)] + [(0, cut, S), (1, cut, S)]
        ):
            weigh(first[:, base : base + 2 * (b - a)].rearrange("p (n s) -> p n s", n=2), t, a, b)
            base = base + 2 * (b - a)

        out_codes = keep.tile([P, S], U32, name="out_codes", align_bytes=64)
        out_scales = keep.tile([P, S], U8, name="out_scales", align_bytes=64)
        out_rows = out_0.rearrange("(p t) c -> p t c", t=PACK)
        out_acc = []
        for j in range(NCH):
            recip = keep.tile([P, H], F32, name="recip%d" % j, tag="recip%d" % j)
            nc.scalar.activation(
                recip[:].rearrange("s (u p e) -> s u p e", u=2, e=2),
                logs[:, j, :, :].rearrange("s (u e) p -> s u p e", u=2), ACT.Exp, scale=-1.0,
            )
            z_rows = keep.tile([P, H], BF16, name="z_rows%d" % j)
            z_turned = bank(j % (NCH - 1), [P, 2, CH], "z_turned%d" % j)
            pairs = z_rows[:].bitcast(F32)
            for view, u0, u1 in num[j]:
                span = slice(u0 * HALF, u1 * HALF)
                nc.vector.tensor_tensor(
                    z_rows[:, span].rearrange("s (u p e) -> s u p e", p=P, e=2),
                    view.rearrange("s (u e) p -> s u p e", e=2),
                    recip[:, span].rearrange("s (u p e) -> s u p e", p=P, e=2), ALU.mult,
                )
                for u in range(u0, u1):
                    nc.tensor.transpose(z_turned[:, u, :], pairs[:, u * P : (u + 1) * P], ident[:])
            if j < 2:
                last = keep.tile([P, 2, CH], F32, name="last%d" % j, tag="recip%d" % j)
                weigh(last[:], 2 + j, cut, S)
            z_grouped = keep.tile([P, CH * PACK], BF16, name="z_grouped%d" % j, align_bytes=64)
            nc.scalar.copy(
                z_grouped[:].bitcast(F32).rearrange("p (s u) -> p s u", u=2),
                z_turned[:].rearrange("p u s -> p s u"),
            )
            z_codes = keep.tile([P, CH], U32, name="z_codes%d" % j, align_bytes=64)
            z_scales = keep.tile([P, CH], U8, name="z_scales%d" % j, align_bytes=64)
            nc.vector.quantize_mx(out=z_codes[:].bitcast(FP8X4), scales=z_scales[:], in_=z_grouped[:])

            acc = pair_views(j, "out_acc%d" % j, NCH - 1)
            for t in range(PACK):
                product(slot(acc, t), w3w, w23s, 4, t, z_codes[:], z_scales[:])
            out_acc.append(acc)

        for j in range(NCH):
            cols = slice(j * CH, (j + 1) * CH)
            result = keep.tile([P, PACK, CH], F32, name="result%d" % j)
            for view, u0, u1 in out_acc[j]:
                nc.scalar.copy(result[:, 2 * u0 : 2 * u1, :], view)
            nc.sync.dma_start(out_rows[:, :, cols], result[:])
            grouped = keep.tile([P, CH * PACK], BF16, name="grouped%d" % j, align_bytes=64)
            nc.vector.tensor_copy(
                grouped[:].rearrange("p (s t) -> p s t", t=PACK), result[:].rearrange("p t s -> p s t")
            )
            nc.vector.quantize_mx(out=out_codes[:, cols].bitcast(FP8X4), scales=out_scales[:, cols], in_=grouped[:])
            nc.sync.dma_start(words_of(out_1)[:, cols], out_codes[:, cols].bitcast(I32))

        scale_rows = out_2[0].bitcast(I32)
        for q in range(4):
            queue = nc.sync if q % 2 == 0 else nc.scalar
            queue.dma_start(scale_rows[4 * q : 4 * q + 4, :], out_scales[32 * q : 32 * q + 4, :].bitcast(I32))
